import numpy as np
import ml_dtypes


def mxq(x, axis, fmt="e4m3"):
    dtype, down = {"e4m3": (ml_dtypes.float8_e4m3fn, 7), "e5m2": (ml_dtypes.float8_e5m2, 14)}[fmt]
    v = np.moveaxis(np.asarray(x, np.float32).astype(ml_dtypes.bfloat16).astype(np.float64), axis, -1)
    blocks = v.reshape(v.shape[:-1] + (-1, 32))
    amax = np.abs(blocks).max(-1, keepdims=True)
    byte = np.maximum(np.where(amax > 0, np.frexp(amax)[1] - 1 + 127, 0) - down, 1)
    scale = np.exp2(byte - 127.0)
    codes = (blocks / scale).astype(np.float32).astype(dtype).astype(np.float64)
    return np.moveaxis((codes * scale).reshape(v.shape), -1, axis)


WIDE = False


def mx_kscale(k):
    if not WIDE:
        return np.ones(k)
    levels = np.array([30, -30])
    if k % 512:
        return np.exp2(np.random.permutation(np.resize(levels, k // 32))).repeat(32)
    a = np.empty((k // 512, 16))
    for p in range(k // 512):
        a[p, :8] = np.random.permutation(np.resize(levels, 8))
        for g in range(8):
            far = levels[np.abs(levels - a[p, g]) >= 10]
            a[p, g + 8] = far[np.random.randint(len(far))]
    return np.exp2(a.ravel()).repeat(32)


def f64(x):
    return np.asarray(x).astype(np.float64)


def striped(idx):
    return np.tile(np.asarray(idx).reshape(-1, 16).T, (8, 1)).astype(np.uint16)


def unstriped(offs):
    return offs[:16].T.reshape(-1).astype(np.int64)


E2M1 = np.array([0.0, 0.5, 1.0, 1.5, 2.0, 3.0, 4.0, 6.0, -0.0, -0.5, -1.0, -1.5, -2.0, -3.0, -4.0, -6.0])


def pack_weight(w, fmt):
    k, n = w.shape
    w = f64(np.asarray(w, np.float32).astype(ml_dtypes.bfloat16)).reshape(k // 32, 32, n)
    amax = np.abs(w).max(1)
    if fmt == "e4m3":
        byte = np.frexp(amax)[1] - 1 + 127 - 7
    else:
        mant, ex = np.frexp(amax / 6.0)
        byte = np.where(mant > 0.5, ex, ex - 1) + 127
    byte = np.clip(np.where(amax > 0, byte, 1), 1, 254)
    scaled = (w * np.exp2(127.0 - byte)[:, None, :]).reshape(k, n).astype(np.float32)
    by_word = np.ascontiguousarray(scaled.reshape(k // 512, 128, 4, n).transpose(0, 1, 3, 2))
    if fmt == "e4m3":
        words = by_word.astype(ml_dtypes.float8_e4m3fn).view(np.uint8)
    else:
        c = by_word.astype(ml_dtypes.float4_e2m1fn).view(np.uint8) & 0xF
        words = (c[..., 0::2] | (c[..., 1::2] << 4)).reshape(k // 512, 128, 2 * n)
    return np.ascontiguousarray(words), np.ascontiguousarray(byte.astype(np.uint8).reshape(k // 512, 16, n))


def unpack_weight(words, scales, fmt):
    g, _, n = scales.shape
    words = np.ascontiguousarray(words).reshape(g, 128, n, -1)
    if fmt == "e4m3":
        vals = words.view(ml_dtypes.float8_e4m3fn).astype(np.float64)
    else:
        nib = np.empty((g, 128, n, 4), np.uint8)
        nib[..., 0::2] = words & 0xF
        nib[..., 1::2] = words >> 4
        vals = E2M1[nib]
    vals = vals * np.repeat(np.exp2(scales.astype(np.float64) - 127.0), 8, axis=1)[..., None]
    return vals.transpose(0, 1, 3, 2).reshape(g * 512, n)


K, T, J, S, R, N, Z = 512, 512, 256, 512, 512, 256, 512


def setup_inputs():
    n = np.random.standard_normal
    idx = np.random.permutation(T)[:J]
    idx2 = np.random.permutation(S)[:J]
    idx3 = np.random.permutation(Z)[:J]
    fk = mx_kscale(K)
    fr = mx_kscale(R)
    wp = pack_weight(n((K, R)) * 1 / np.sqrt(K) * fk[:, None], "e2m1")
    wbp = pack_weight(n((R, N)) * 1 / np.sqrt(R) / fr[:, None], "e2m1")
    return {
        "xa": (n((K, T))).astype(np.float32),
        "xb": (n((K, S))).astype(np.float32),
        "hb": (np.random.uniform(0.2, 0.9, (K, 1))).astype(np.float32),
        "fk": (np.random.uniform(0.5, 2.0, (K, 1)) / fk[:, None]).astype(np.float32),
        "w_words": wp[0],
        "w_scales": wp[1],
        "us": (np.random.uniform(0.5, 1.5, (1, R)) * fr).astype(np.float32),
        "wb_words": wbp[0],
        "wb_scales": wbp[1],
        "tz": (n((N, Z)) * 0.6).astype(np.float32),
        "rw": (np.random.uniform(0.5, 2.0, (1, J))).astype(np.float32),
        "offs": striped(idx),
        "offs2": striped(idx2),
        "offs3": striped(idx3),
    }


def reference(xa, xb, hb, fk, w_words, w_scales, us, wb_words, wb_scales, tz, rw, offs, offs2, offs3):
    idx = unstriped(offs)
    idx2 = unstriped(offs2)
    idx3 = unstriped(offs3)
    wu = unpack_weight(w_words, w_scales, "e2m1")
    wbu = unpack_weight(wb_words, wb_scales, "e2m1")
    u = (f64(xa)[:, idx] - np.minimum(f64(xb)[:, idx2], f64(hb))) * f64(fk)
    uq = mxq(u, 0, "e4m3")
    a = uq.T @ wu
    m1 = np.pad(a, ((0, 0), (1, 0)))[:, :R]
    hr = (a - 0.7 * m1) * f64(us)
    hid = hr.T
    hidq = mxq(hid, 0, "e5m2")
    p = wbu.T @ hidq
    y = np.maximum(p, f64(tz)[:, idx3]) * f64(rw)
    return y

@@ -1,0 +1,177 @@
+from contextlib import ExitStack
+
+import concourse.mybir as mybir
+
+K, T, J, S, R, N, Z = 512, 512, 256, 512, 512, 256, 512
+FLOPS = 2 * K * J * R + 2 * R * N * J
+
+F32 = mybir.dt.float32
+BF16 = mybir.dt.bfloat16
+I32 = mybir.dt.int32
+U32 = mybir.dt.uint32
+U16 = mybir.dt.uint16
+U8 = mybir.dt.uint8
+E4M3 = mybir.dt.float8_e4m3fn_x4
+E5M2 = mybir.dt.float8_e5m2_x4
+E2M1 = mybir.dt.float4_e2m1fn_x4
+ALU = mybir.AluOpType
+COPY = mybir.ActivationFunctionType.Copy
+
+P = 128
+PACK = 4
+HALF = J // 2
+NEIGHBOUR = 0.7
+
+
+def tile_list_rows_boundedgaps_neighbours_floored_kernel(
+    tc, xa, xb, hb, fk, w_words, w_scales, us, wb_words, wb_scales, tz, rw, offs, offs2, offs3, out
+):
+    nc = tc.nc
+    with ExitStack() as ctx:
+        lists = ctx.enter_context(tc.tile_pool(name="lists", bufs=1))
+        sb = ctx.enter_context(tc.tile_pool(name="sb", bufs=1))
+        ps = ctx.enter_context(tc.psum_pool(name="ps", bufs=1))
+
+        list_a = lists.tile([P, J // 16], U16, name="list_a")
+        list_b = lists.tile([P, J // 16], U16, name="list_b")
+        list_z = lists.tile([P, J // 16], U16, name="list_z")
+
+        xa_rows = xa.rearrange("(p i) t -> p i t", i=PACK)
+        xb_rows = xb.rearrange("(p i) s -> p (i s)", i=PACK)
+        xa_sb = [sb.tile([P, T], F32, name="xa%d" % i) for i in range(PACK)]
+        xb_sb = [sb.tile([P, 2 * S], F32, name="xb%d" % g) for g in range(2)]
+        tz_sb = sb.tile([P, 2 * Z], F32, name="tz_sb")
+        hb_sb = sb.tile([P, PACK], F32, name="hb_sb")
+        fk_sb = sb.tile([P, PACK], F32, name="fk_sb")
+        us_sb = sb.tile([P, PACK], F32, name="us_sb")
+        rw_sb = sb.tile([P, J], F32, name="rw_sb")
+        w_raw = sb.tile([P, 2 * R], U8, name="w_raw", align_bytes=64)
+        ws_raw = sb.tile([P, R], U8, name="ws_raw", align_bytes=64)
+        wb_sb = sb.tile([P, 2 * N], U8, name="wb_sb", align_bytes=64)
+        wbs_sb = sb.tile([P, N], U8, name="wbs_sb", align_bytes=64)
+
+
+        nc.sync.dma_start(list_b[:], offs2)
+        nc.sync.dma_start(list_a[:], offs)
+        nc.sync.dma_start(xb_sb[0][:], xb_rows[:, 0 : 2 * S])
+        ws_rows = w_scales[0].bitcast(I32)
+        for q in range(4):
+            rows = ws_rows[4 * q : 4 * q + 4, :].unsqueeze(0).to_broadcast([8, 4, R // 4])
+            nc.scalar.dma_start(ws_raw[32 * q : 32 * q + 32, :].bitcast(I32), rows)
+        nc.sync.dma_start(xb_sb[1][:], xb_rows[:, 2 * S : 4 * S])
+        nc.gpsimd.dma_start(hb_sb[:], hb.rearrange("(p i) o -> p (i o)", i=PACK))
+        nc.gpsimd.dma_start(fk_sb[:], fk.rearrange("(p i) o -> p (i o)", i=PACK))
+        nc.gpsimd.dma_start(us_sb[:], us.rearrange("o (p t) -> p (o t)", t=PACK))
+        for i in range(PACK):
+            nc.sync.dma_start(xa_sb[i][:], xa_rows[:, i, :])
+        nc.sync.dma_start(w_raw[:], w_words[0])
+        nc.sync.dma_start(list_z[:], offs3)
+        nc.sync.dma_start(
+            tz_sb[:].rearrange("p (h z) -> p h z", h=2), tz.rearrange("(h p) z -> p h z", h=2)
+        )
+        nc.sync.dma_start(wb_sb[:], wb_words[0])
+        wbs_rows = wb_scales[0].bitcast(I32)
+        nc.gpsimd.memset(wbs_sb[:].bitcast(I32), 0)
+        for r in range(4):
+            nc.gpsimd.dma_start(wbs_sb[r:P:32, :].bitcast(I32), wbs_rows[r:16:4, :])
+        nc.sync.dma_start(rw_sb[:], rw.to_broadcast([P, J]))
+
+        ws_dealt = sb.tile([P, 5 * P], U8, name="ws_dealt", align_bytes=64)
+        nc.gpsimd.memset(ws_dealt[:, 0:4].bitcast(I32), 0)
+        nc.vector.tensor_copy(ws_dealt[:, 1:P], ws_raw[:, PACK - 1 : R - PACK : PACK])
+        nc.vector.tensor_copy(
+            ws_dealt[:, P:].rearrange("p (t m) -> p t m", t=PACK),
+            ws_raw[:].rearrange("p (m t) -> p t m", t=PACK),
+        )
+
+        gb = [sb.tile([P, J], F32, name="gb%d" % i) for i in range(PACK)]
+        low = [sb.tile([P, J], F32, name="low%d" % i) for i in range(PACK)]
+        gap = [sb.tile([P, J], F32, name="gap%d" % i) for i in range(PACK)]
+        u_bf = sb.tile([P, PACK * J], BF16, name="u_bf", align_bytes=64)
+        for i in range(PACK):
+            window = xb_sb[i // 2][:, (i % 2) * S : (i % 2 + 1) * S].indirect(list_b[:])
+            if i % 2 == 0:
+                nc.scalar.activation(gb[i][:], window, COPY)
+            else:
+                nc.vector.tensor_copy(gb[i][:], window)
+        for i in range(PACK):
+            nc.vector.tensor_scalar(low[i][:], gb[i][:], hb_sb[:, i : i + 1], None, op0=ALU.min)
+        for i in range(PACK):
+            nc.vector.tensor_tensor(gap[i][:], xa_sb[i][:].indirect(list_a[:]), low[i][:], ALU.subtract)
+            if i < 2:
+                nc.scalar.activation(u_bf[:, i : PACK * J : PACK], gap[i][:], COPY, scale=fk_sb[:, i : i + 1])
+        for i in range(2, PACK):
+            nc.vector.tensor_scalar(
+                u_bf[:, i : PACK * J : PACK], gap[i][:], fk_sb[:, i : i + 1], None, op0=ALU.mult
+            )
+        u_codes = sb.tile([P, J], U32, name="u_codes", align_bytes=64)
+        u_scales = sb.tile([P, J], U8, name="u_scales", align_bytes=64)
+        nc.vector.quantize_mx(out=u_codes[:].bitcast(E4M3), scales=u_scales[:], in_=u_bf[:])
+
+        w_dealt = sb.tile([P, 5 * 2 * P], U8, name="w_dealt", align_bytes=64)
+        w16 = w_raw[:].bitcast(U16)
+        d16 = w_dealt[:].bitcast(U16)
+        nc.gpsimd.memset(w_dealt[:, 0:4].bitcast(I32), 0)
+        nc.scalar.copy(d16[:, 1:P], w16[:, PACK - 1 : R - PACK : PACK])
+        nc.scalar.copy(
+            d16[:, P:].rearrange("p (t m) -> p t m", t=PACK),
+            w16.rearrange("p (m t) -> p t m", t=PACK),
+        )
+
+        us_neg = sb.tile([P, PACK], F32, name="us_neg")
+        nc.vector.tensor_scalar(us_neg[:], us_sb[:], -NEIGHBOUR, None, op0=ALU.mult)
+
+        tz_g = sb.tile([P, 2, J], F32, name="tz_g")
+        for h in range(2):
+            nc.scalar.activation(tz_g[:, h, :], tz_sb[:, h * Z : (h + 1) * Z].indirect(list_z[:]), COPY)
+
+        acc = [ps.tile([P, J], F32, name="acc%d" % s) for s in range(5)]
+        for s in (3, 4, 2, 1, 0):
+            nc.tensor.matmul_mx(
+                out=acc[s][:],
+                lhsT=w_dealt[:, 2 * P * s : 2 * P * (s + 1)].bitcast(E2M1),
+                lhsT_scale=ws_dealt[:, P * s : P * (s + 1)],
+                rhs=u_codes[:].bitcast(E4M3),
+                rhs_scale=u_scales[:],
+                start=True,
+                stop=True,
+            )
+
+        before = [sb.tile([P, J], F32, name="before%d" % t) for t in range(PACK)]
+        hid_planes = sb.tile([P, PACK, J], BF16, name="hid_planes")
+        for t in reversed(range(PACK)):
+            nc.scalar.activation(before[t][:], acc[t][:], COPY, scale=us_neg[:, t : t + 1])
+            nc.vector.scalar_tensor_tensor(
+                hid_planes[:, t, :], acc[t + 1][:], us_sb[:, t : t + 1], before[t][:], op0=ALU.mult, op1=ALU.add
+            )
+
+        hid_bf = [sb.tile([P, PACK * HALF], BF16, name="hid_bf%d" % g, align_bytes=64) for g in range(2)]
+        hid_codes = [sb.tile([P, HALF], U32, name="hid_codes%d" % g, align_bytes=64) for g in range(2)]
+        hid_scales = [sb.tile([P, HALF], U8, name="hid_scales%d" % g, align_bytes=64) for g in range(2)]
+        second = [ps.tile([P, 2, HALF], F32, name="second%d" % g) for g in range(2)]
+        top = [sb.tile([P, 2, HALF], F32, name="top%d" % g) for g in range(2)]
+        y = [sb.tile([P, 2, HALF], F32, name="y%d" % g) for g in range(2)]
+        out_rows = out.rearrange("(h p) j -> p h j", h=2)
+        for g in range(2):
+            nc.vector.tensor_copy(
+                hid_bf[g][:].rearrange("p (j t) -> p j t", t=PACK),
+                hid_planes[:, :, g * HALF : (g + 1) * HALF].rearrange("p t j -> p j t"),
+            )
+        for g in range(2):
+            nc.vector.quantize_mx(out=hid_codes[g][:].bitcast(E5M2), scales=hid_scales[g][:], in_=hid_bf[g][:])
+            for h in range(2):
+                nc.tensor.matmul_mx(
+                    out=second[g][:, h, :],
+                    lhsT=wb_sb[:, 2 * P * h : 2 * P * (h + 1)].bitcast(E2M1),
+                    lhsT_scale=wbs_sb[:, P * h : P * (h + 1)],
+                    rhs=hid_codes[g][:].bitcast(E5M2),
+                    rhs_scale=hid_scales[g][:],
+                    start=True,
+                    stop=True,
+                )
+        for g in range(2):
+            nc.vector.tensor_tensor(top[g][:], second[g][:], tz_g[:, :, g * HALF : (g + 1) * HALF], ALU.max)
+        for g in range(2):
+            weight = rw_sb[:, g * HALF : (g + 1) * HALF].unsqueeze(1).to_broadcast([P, 2, HALF])
+            nc.vector.tensor_tensor(y[g][:], top[g][:], weight, ALU.mult)
+            nc.sync.dma_start(out_rows[:, :, g * HALF : (g + 1) * HALF], y[g][:])

@@ -21,6 +21,21 @@ P = 128
 PACK = 4
 HALF = J // 2
 NEIGHBOUR = 0.7
+SLOTS = PACK + 1
+
+
+def load_scale_rows(queue, plane, scales):
+    rows = scales[0].bitcast(I32)
+    for q in range(4):
+        four = rows[4 * q : 4 * q + 4, :].unsqueeze(0).to_broadcast([8, 4, rows.shape[1]])
+        queue.dma_start(plane[32 * q : 32 * q + 32, :].bitcast(I32), four)
+
+
+def interleave(nc, packed, planes):
+    nc.vector.tensor_copy(
+        packed.rearrange("p (c i t) -> p c t i", i=4, t=PACK),
+        planes.rearrange("p t (c i) -> p c t i", i=4),
+    )
 
 
 def tile_list_rows_boundedgaps_neighbours_floored_kernel(
@@ -31,6 +46,7 @@ def tile_list_rows_boundedgaps_neighbours_floored_kernel(
         lists = ctx.enter_context(tc.tile_pool(name="lists", bufs=1))
         sb = ctx.enter_context(tc.tile_pool(name="sb", bufs=1))
         ps = ctx.enter_context(tc.psum_pool(name="ps", bufs=1))
+        halves = [slice(g * HALF, (g + 1) * HALF) for g in range(2)]
 
         list_a = lists.tile([P, J // 16], U16, name="list_a")
         list_b = lists.tile([P, J // 16], U16, name="list_b")
@@ -50,34 +66,27 @@ def tile_list_rows_boundedgaps_neighbours_floored_kernel(
         wb_sb = sb.tile([P, 2 * N], U8, name="wb_sb", align_bytes=64)
         wbs_sb = sb.tile([P, N], U8, name="wbs_sb", align_bytes=64)
 
-
         nc.sync.dma_start(list_b[:], offs2)
         nc.sync.dma_start(list_a[:], offs)
         nc.sync.dma_start(xb_sb[0][:], xb_rows[:, 0 : 2 * S])
-        ws_rows = w_scales[0].bitcast(I32)
-        for q in range(4):
-            rows = ws_rows[4 * q : 4 * q + 4, :].unsqueeze(0).to_broadcast([8, 4, R // 4])
-            nc.scalar.dma_start(ws_raw[32 * q : 32 * q + 32, :].bitcast(I32), rows)
+        load_scale_rows(nc.sync, ws_raw, w_scales)
         nc.sync.dma_start(xb_sb[1][:], xb_rows[:, 2 * S : 4 * S])
         nc.gpsimd.dma_start(hb_sb[:], hb.rearrange("(p i) o -> p (i o)", i=PACK))
         nc.gpsimd.dma_start(fk_sb[:], fk.rearrange("(p i) o -> p (i o)", i=PACK))
-        nc.gpsimd.dma_start(us_sb[:], us.rearrange("o (p t) -> p (o t)", t=PACK))
         for i in range(PACK):
             nc.sync.dma_start(xa_sb[i][:], xa_rows[:, i, :])
         nc.sync.dma_start(w_raw[:], w_words[0])
         nc.sync.dma_start(list_z[:], offs3)
+        nc.sync.dma_start(us_sb[:], us.rearrange("o (p t) -> p (o t)", t=PACK))
         nc.sync.dma_start(
             tz_sb[:].rearrange("p (h z) -> p h z", h=2), tz.rearrange("(h p) z -> p h z", h=2)
         )
         nc.sync.dma_start(wb_sb[:], wb_words[0])
-        wbs_rows = wb_scales[0].bitcast(I32)
-        nc.gpsimd.memset(wbs_sb[:].bitcast(I32), 0)
-        for r in range(4):
-            nc.gpsimd.dma_start(wbs_sb[r:P:32, :].bitcast(I32), wbs_rows[r:16:4, :])
+        load_scale_rows(nc.sync, wbs_sb, wb_scales)
         nc.sync.dma_start(rw_sb[:], rw.to_broadcast([P, J]))
 
-        ws_dealt = sb.tile([P, 5 * P], U8, name="ws_dealt", align_bytes=64)
-        nc.gpsimd.memset(ws_dealt[:, 0:4].bitcast(I32), 0)
+        ws_dealt = sb.tile([P, SLOTS * P], U8, name="ws_dealt", align_bytes=64)
+        nc.vector.memset(ws_dealt[:, 0:4].bitcast(I32), 0)
         nc.vector.tensor_copy(ws_dealt[:, 1:P], ws_raw[:, PACK - 1 : R - PACK : PACK])
         nc.vector.tensor_copy(
             ws_dealt[:, P:].rearrange("p (t m) -> p t m", t=PACK),
@@ -86,92 +95,102 @@ def tile_list_rows_boundedgaps_neighbours_floored_kernel(
 
         gb = [sb.tile([P, J], F32, name="gb%d" % i) for i in range(PACK)]
         low = [sb.tile([P, J], F32, name="low%d" % i) for i in range(PACK)]
-        gap = [sb.tile([P, J], F32, name="gap%d" % i) for i in range(PACK)]
-        u_bf = sb.tile([P, PACK * J], BF16, name="u_bf", align_bytes=64)
         for i in range(PACK):
             window = xb_sb[i // 2][:, (i % 2) * S : (i % 2 + 1) * S].indirect(list_b[:])
-            if i % 2 == 0:
+            if i != 2:
                 nc.scalar.activation(gb[i][:], window, COPY)
             else:
                 nc.vector.tensor_copy(gb[i][:], window)
         for i in range(PACK):
-            nc.vector.tensor_scalar(low[i][:], gb[i][:], hb_sb[:, i : i + 1], None, op0=ALU.min)
-        for i in range(PACK):
-            nc.vector.tensor_tensor(gap[i][:], xa_sb[i][:].indirect(list_a[:]), low[i][:], ALU.subtract)
-            if i < 2:
-                nc.scalar.activation(u_bf[:, i : PACK * J : PACK], gap[i][:], COPY, scale=fk_sb[:, i : i + 1])
-        for i in range(2, PACK):
             nc.vector.tensor_scalar(
-                u_bf[:, i : PACK * J : PACK], gap[i][:], fk_sb[:, i : i + 1], None, op0=ALU.mult
+                low[i][:], gb[i][:], hb_sb[:, i : i + 1], fk_sb[:, i : i + 1], op0=ALU.min, op1=ALU.mult
             )
-        u_codes = sb.tile([P, J], U32, name="u_codes", align_bytes=64)
-        u_scales = sb.tile([P, J], U8, name="u_scales", align_bytes=64)
-        nc.vector.quantize_mx(out=u_codes[:].bitcast(E4M3), scales=u_scales[:], in_=u_bf[:])
 
-        w_dealt = sb.tile([P, 5 * 2 * P], U8, name="w_dealt", align_bytes=64)
+        u_planes = sb.tile([P, PACK, J], BF16, name="u_planes")
+        pieces = [(i, 0, J) for i in range(PACK - 1)] + [(PACK - 1, 0, HALF), (PACK - 1, HALF, J)]
+        for n, (i, j0, j1) in enumerate(pieces):
+            ga = sb.tile([P, j1 - j0], F32, name="ga%d" % n, tag="ga%d" % n, align_bytes=64)
+            window = xa_sb[i][:].indirect(list_a[:, j0 // 16 : j1 // 16])
+            if n in (0, 4):
+                nc.vector.tensor_copy(ga[:], window)
+            else:
+                nc.scalar.activation(ga[:], window, COPY)
+            nc.vector.scalar_tensor_tensor(
+                u_planes[:, i, j0:j1], ga[:], fk_sb[:, i : i + 1], low[i][:, j0:j1], op0=ALU.mult, op1=ALU.subtract
+            )
+
+        u_bf = [sb.tile([P, PACK * HALF], BF16, name="u_bf%d" % g, align_bytes=64) for g in range(2)]
+        u_codes = [sb.tile([P, HALF], U32, name="u_codes%d" % g, align_bytes=64) for g in range(2)]
+        u_scales = [sb.tile([P, HALF], U8, name="u_scales%d" % g, align_bytes=64) for g in range(2)]
+        for g in range(2):
+            interleave(nc, u_bf[g][:], u_planes[:, :, halves[g]])
+        for g in range(2):
+            nc.vector.quantize_mx(out=u_codes[g][:].bitcast(E4M3), scales=u_scales[g][:], in_=u_bf[g][:])
+
+        w_dealt = sb.tile([P, SLOTS * 2 * P], U8, name="w_dealt", tag="ga3", align_bytes=64)
         w16 = w_raw[:].bitcast(U16)
         d16 = w_dealt[:].bitcast(U16)
-        nc.gpsimd.memset(w_dealt[:, 0:4].bitcast(I32), 0)
-        nc.scalar.copy(d16[:, 1:P], w16[:, PACK - 1 : R - PACK : PACK])
         nc.scalar.copy(
             d16[:, P:].rearrange("p (t m) -> p t m", t=PACK),
             w16.rearrange("p (m t) -> p t m", t=PACK),
         )
+        nc.gpsimd.memset(w_dealt[:, 0:4].bitcast(I32), 0)
+        nc.scalar.copy(d16[:, 1:P], w16[:, PACK - 1 : R - PACK : PACK])
 
         us_neg = sb.tile([P, PACK], F32, name="us_neg")
-        nc.vector.tensor_scalar(us_neg[:], us_sb[:], -NEIGHBOUR, None, op0=ALU.mult)
+        nc.gpsimd.tensor_scalar(us_neg[:], us_sb[:], -NEIGHBOUR, None, op0=ALU.mult)
 
-        tz_g = sb.tile([P, 2, J], F32, name="tz_g")
-        for h in range(2):
-            nc.scalar.activation(tz_g[:, h, :], tz_sb[:, h * Z : (h + 1) * Z].indirect(list_z[:]), COPY)
+        tz_g = sb.tile([P, 2, J], F32, name="tz_g", tag="ga4", align_bytes=64)
+        nc.scalar.activation(tz_g[:, 0, :], tz_sb[:, 0:Z].indirect(list_z[:]), COPY)
 
-        acc = [ps.tile([P, J], F32, name="acc%d" % s) for s in range(5)]
-        for s in (3, 4, 2, 1, 0):
-            nc.tensor.matmul_mx(
-                out=acc[s][:],
-                lhsT=w_dealt[:, 2 * P * s : 2 * P * (s + 1)].bitcast(E2M1),
-                lhsT_scale=ws_dealt[:, P * s : P * (s + 1)],
-                rhs=u_codes[:].bitcast(E4M3),
-                rhs_scale=u_scales[:],
-                start=True,
-                stop=True,
-            )
-
-        before = [sb.tile([P, J], F32, name="before%d" % t) for t in range(PACK)]
-        hid_planes = sb.tile([P, PACK, J], BF16, name="hid_planes")
-        for t in reversed(range(PACK)):
-            nc.scalar.activation(before[t][:], acc[t][:], COPY, scale=us_neg[:, t : t + 1])
-            nc.vector.scalar_tensor_tensor(
-                hid_planes[:, t, :], acc[t + 1][:], us_sb[:, t : t + 1], before[t][:], op0=ALU.mult, op1=ALU.add
-            )
-
-        hid_bf = [sb.tile([P, PACK * HALF], BF16, name="hid_bf%d" % g, align_bytes=64) for g in range(2)]
-        hid_codes = [sb.tile([P, HALF], U32, name="hid_codes%d" % g, align_bytes=64) for g in range(2)]
-        hid_scales = [sb.tile([P, HALF], U8, name="hid_scales%d" % g, align_bytes=64) for g in range(2)]
-        second = [ps.tile([P, 2, HALF], F32, name="second%d" % g) for g in range(2)]
-        top = [sb.tile([P, 2, HALF], F32, name="top%d" % g) for g in range(2)]
-        y = [sb.tile([P, 2, HALF], F32, name="y%d" % g) for g in range(2)]
         out_rows = out.rearrange("(h p) j -> p h j", h=2)
+        acc = []
+        second = []
         for g in range(2):
-            nc.vector.tensor_copy(
-                hid_bf[g][:].rearrange("p (j t) -> p j t", t=PACK),
-                hid_planes[:, :, g * HALF : (g + 1) * HALF].rearrange("p t j -> p j t"),
-            )
+            banks = [ps.tile([P, 2, HALF], F32, name="first%d_%d" % (g, b)) for b in range(3)]
+            acc.append([banks[(s + 1) // 2][:, s % 2, :] for s in range(SLOTS)])
+            for s in (3, 4, 2, 1, 0):
+                nc.tensor.matmul_mx(
+                    out=acc[g][s],
+                    lhsT=w_dealt[:, 2 * P * s : 2 * P * (s + 1)].bitcast(E2M1),
+                    lhsT_scale=ws_dealt[:, P * s : P * (s + 1)],
+                    rhs=u_codes[g][:].bitcast(E4M3),
+                    rhs_scale=u_scales[g][:],
+                    start=True,
+                    stop=True,
+                )
         for g in range(2):
-            nc.vector.quantize_mx(out=hid_codes[g][:].bitcast(E5M2), scales=hid_scales[g][:], in_=hid_bf[g][:])
+            hid_planes = sb.tile([P, PACK, HALF], BF16, name="hid_planes%d" % g)
+            for t in reversed(range(PACK)):
+                if (g, t) == (1, PACK - 1):
+                    before = tz_g[:, 1, 0:HALF]
+                else:
+                    before = sb.tile([P, HALF], F32, name="before%d_%d" % (g, t))[:]
+                nc.scalar.activation(before, acc[g][t], COPY, scale=us_neg[:, t : t + 1])
+                nc.vector.scalar_tensor_tensor(
+                    hid_planes[:, t, :], acc[g][t + 1], us_sb[:, t : t + 1], before, op0=ALU.mult, op1=ALU.add
+                )
+            hid_bf = sb.tile([P, PACK * HALF], BF16, name="hid_bf%d" % g, align_bytes=64)
+            hid_codes = sb.tile([P, HALF], U32, name="hid_codes%d" % g, align_bytes=64)
+            hid_scales = sb.tile([P, HALF], U8, name="hid_scales%d" % g, align_bytes=64)
+            interleave(nc, hid_bf[:], hid_planes[:])
+            nc.vector.quantize_mx(out=hid_codes[:].bitcast(E5M2), scales=hid_scales[:], in_=hid_bf[:])
+            second.append(ps.tile([P, 2, HALF], F32, name="second%d" % g))
             for h in range(2):
                 nc.tensor.matmul_mx(
                     out=second[g][:, h, :],
                     lhsT=wb_sb[:, 2 * P * h : 2 * P * (h + 1)].bitcast(E2M1),
                     lhsT_scale=wbs_sb[:, P * h : P * (h + 1)],
-                    rhs=hid_codes[g][:].bitcast(E5M2),
-                    rhs_scale=hid_scales[g][:],
+                    rhs=hid_codes[:].bitcast(E5M2),
+                    rhs_scale=hid_scales[:],
                     start=True,
                     stop=True,
                 )
+        nc.scalar.activation(tz_g[:, 1, :], tz_sb[:, Z : 2 * Z].indirect(list_z[:]), COPY)
         for g in range(2):
-            nc.vector.tensor_tensor(top[g][:], second[g][:], tz_g[:, :, g * HALF : (g + 1) * HALF], ALU.max)
-        for g in range(2):
-            weight = rw_sb[:, g * HALF : (g + 1) * HALF].unsqueeze(1).to_broadcast([P, 2, HALF])
-            nc.vector.tensor_tensor(y[g][:], top[g][:], weight, ALU.mult)
-            nc.sync.dma_start(out_rows[:, :, g * HALF : (g + 1) * HALF], y[g][:])
+            top = sb.tile([P, 2, HALF], F32, name="top%d" % g)
+            y = sb.tile([P, 2, HALF], F32, name="y%d" % g)
+            nc.vector.tensor_tensor(top[:], second[g][:], tz_g[:, :, halves[g]], ALU.max)
+            weight = rw_sb[:, halves[g]].unsqueeze(1).to_broadcast([P, 2, HALF])
+            nc.vector.tensor_tensor(y[:], top[:], weight, ALU.mult)
+            nc.sync.dma_start(out_rows[:, :, halves[g]], y[:])

@@ -31,8 +31,8 @@ def load_scale_rows(queue, plane, scales):
         queue.dma_start(plane[32 * q : 32 * q + 32, :].bitcast(I32), four)
 
 
-def interleave(nc, packed, planes):
-    nc.vector.tensor_copy(
+def interleave(copy, packed, planes):
+    copy(
         packed.rearrange("p (c i t) -> p c t i", i=4, t=PACK),
         planes.rearrange("p t (c i) -> p c t i", i=4),
     )
@@ -67,13 +67,14 @@ def tile_list_rows_boundedgaps_neighbours_floored_kernel(
         wbs_sb = sb.tile([P, N], U8, name="wbs_sb", align_bytes=64)
 
         nc.sync.dma_start(list_b[:], offs2)
-        nc.sync.dma_start(list_a[:], offs)
-        nc.sync.dma_start(xb_sb[0][:], xb_rows[:, 0 : 2 * S])
         load_scale_rows(nc.sync, ws_raw, w_scales)
+        nc.sync.dma_start(xb_sb[0][:], xb_rows[:, 0 : 2 * S])
         nc.sync.dma_start(xb_sb[1][:], xb_rows[:, 2 * S : 4 * S])
+        nc.sync.dma_start(xa_sb[0][:], xa_rows[:, 0, :])
+        nc.sync.dma_start(list_a[:], offs)
         nc.gpsimd.dma_start(hb_sb[:], hb.rearrange("(p i) o -> p (i o)", i=PACK))
         nc.gpsimd.dma_start(fk_sb[:], fk.rearrange("(p i) o -> p (i o)", i=PACK))
-        for i in range(PACK):
+        for i in range(1, PACK):
             nc.sync.dma_start(xa_sb[i][:], xa_rows[:, i, :])
         nc.sync.dma_start(w_raw[:], w_words[0])
         nc.sync.dma_start(list_z[:], offs3)
@@ -97,7 +98,7 @@ def tile_list_rows_boundedgaps_neighbours_floored_kernel(
         low = [sb.tile([P, J], F32, name="low%d" % i) for i in range(PACK)]
         for i in range(PACK):
             window = xb_sb[i // 2][:, (i % 2) * S : (i % 2 + 1) * S].indirect(list_b[:])
-            if i != 2:
+            if i % 2 == 1:
                 nc.scalar.activation(gb[i][:], window, COPY)
             else:
                 nc.vector.tensor_copy(gb[i][:], window)
@@ -123,7 +124,7 @@ def tile_list_rows_boundedgaps_neighbours_floored_kernel(
         u_codes = [sb.tile([P, HALF], U32, name="u_codes%d" % g, align_bytes=64) for g in range(2)]
         u_scales = [sb.tile([P, HALF], U8, name="u_scales%d" % g, align_bytes=64) for g in range(2)]
         for g in range(2):
-            interleave(nc, u_bf[g][:], u_planes[:, :, halves[g]])
+            interleave(nc.vector.tensor_copy, u_bf[g][:], u_planes[:, :, halves[g]])
         for g in range(2):
             nc.vector.quantize_mx(out=u_codes[g][:].bitcast(E4M3), scales=u_scales[g][:], in_=u_bf[g][:])
 
@@ -159,8 +160,8 @@ def tile_list_rows_boundedgaps_neighbours_floored_kernel(
                     start=True,
                     stop=True,
                 )
+        hid_planes = [sb.tile([P, PACK, HALF], BF16, name="hid_planes%d" % g) for g in range(2)]
         for g in range(2):
-            hid_planes = sb.tile([P, PACK, HALF], BF16, name="hid_planes%d" % g)
             for t in reversed(range(PACK)):
                 if (g, t) == (1, PACK - 1):
                     before = tz_g[:, 1, 0:HALF]
@@ -168,12 +169,13 @@ def tile_list_rows_boundedgaps_neighbours_floored_kernel(
                     before = sb.tile([P, HALF], F32, name="before%d_%d" % (g, t))[:]
                 nc.scalar.activation(before, acc[g][t], COPY, scale=us_neg[:, t : t + 1])
                 nc.vector.scalar_tensor_tensor(
-                    hid_planes[:, t, :], acc[g][t + 1], us_sb[:, t : t + 1], before, op0=ALU.mult, op1=ALU.add
+                    hid_planes[g][:, t, :], acc[g][t + 1], us_sb[:, t : t + 1], before, op0=ALU.mult, op1=ALU.add
                 )
-            hid_bf = sb.tile([P, PACK * HALF], BF16, name="hid_bf%d" % g, align_bytes=64)
+        for g, copy in enumerate((nc.scalar.copy, nc.vector.tensor_copy)):
+            hid_bf = sb.tile([P, PACK * HALF], BF16, name="hid_bf%d" % g, tag="hid_bf%d" % g, align_bytes=64)
             hid_codes = sb.tile([P, HALF], U32, name="hid_codes%d" % g, align_bytes=64)
             hid_scales = sb.tile([P, HALF], U8, name="hid_scales%d" % g, align_bytes=64)
-            interleave(nc, hid_bf[:], hid_planes[:])
+            interleave(copy, hid_bf[:], hid_planes[g][:])
             nc.vector.quantize_mx(out=hid_codes[:].bitcast(E5M2), scales=hid_scales[:], in_=hid_bf[:])
             second.append(ps.tile([P, 2, HALF], F32, name="second%d" % g))
             for h in range(2):
@@ -188,7 +190,7 @@ def tile_list_rows_boundedgaps_neighbours_floored_kernel(
                 )
         nc.scalar.activation(tz_g[:, 1, :], tz_sb[:, Z : 2 * Z].indirect(list_z[:]), COPY)
         for g in range(2):
-            top = sb.tile([P, 2, HALF], F32, name="top%d" % g)
+            top = sb.tile([P, 2, HALF], F32, name="top%d" % g, tag="hid_bf%d" % (1 - g), align_bytes=64)
             y = sb.tile([P, 2, HALF], F32, name="y%d" % g)
             nc.vector.tensor_tensor(top[:], second[g][:], tz_g[:, :, halves[g]], ALU.max)
             weight = rw_sb[:, halves[g]].unsqueeze(1).to_broadcast([P, 2, HALF])

@@ -20,21 +20,22 @@ COPY = mybir.ActivationFunctionType.Copy
 P = 128
 PACK = 4
 HALF = J // 2
+LIST_ROWS = 16
+SETS = PACK + 1
 NEIGHBOUR = 0.7
-SLOTS = PACK + 1
 
 
-def load_scale_rows(queue, plane, scales):
+def load_scale_rows(nc, plane, scales):
     rows = scales[0].bitcast(I32)
     for q in range(4):
         four = rows[4 * q : 4 * q + 4, :].unsqueeze(0).to_broadcast([8, 4, rows.shape[1]])
-        queue.dma_start(plane[32 * q : 32 * q + 32, :].bitcast(I32), four)
+        nc.sync.dma_start(plane[32 * q : 32 * q + 32, :].bitcast(I32), four)
 
 
 def interleave(copy, packed, planes):
     copy(
-        packed.rearrange("p (c i t) -> p c t i", i=4, t=PACK),
-        planes.rearrange("p t (c i) -> p c t i", i=4),
+        packed.rearrange("p (c e t) -> p c t e", e=4, t=PACK),
+        planes.rearrange("p t (c e) -> p c t e", e=4),
     )
 
 
@@ -48,9 +49,9 @@ def tile_list_rows_boundedgaps_neighbours_floored_kernel(
         ps = ctx.enter_context(tc.psum_pool(name="ps", bufs=1))
         halves = [slice(g * HALF, (g + 1) * HALF) for g in range(2)]
 
-        list_a = lists.tile([P, J // 16], U16, name="list_a")
-        list_b = lists.tile([P, J // 16], U16, name="list_b")
-        list_z = lists.tile([P, J // 16], U16, name="list_z")
+        list_a = lists.tile([P, J // LIST_ROWS], U16, name="list_a")
+        list_b = lists.tile([P, J // LIST_ROWS], U16, name="list_b")
+        list_z = lists.tile([P, J // LIST_ROWS], U16, name="list_z")
 
         xa_rows = xa.rearrange("(p i) t -> p i t", i=PACK)
         xb_rows = xb.rearrange("(p i) s -> p (i s)", i=PACK)
@@ -66,27 +67,29 @@ def tile_list_rows_boundedgaps_neighbours_floored_kernel(
         wb_sb = sb.tile([P, 2 * N], U8, name="wb_sb", align_bytes=64)
         wbs_sb = sb.tile([P, N], U8, name="wbs_sb", align_bytes=64)
 
+        nc.sync.dma_start(us_sb[:], us.rearrange("o (p t) -> p (o t)", t=PACK))
         nc.sync.dma_start(list_b[:], offs2)
-        load_scale_rows(nc.sync, ws_raw, w_scales)
+        load_scale_rows(nc, ws_raw, w_scales)
         nc.sync.dma_start(xb_sb[0][:], xb_rows[:, 0 : 2 * S])
         nc.sync.dma_start(xb_sb[1][:], xb_rows[:, 2 * S : 4 * S])
-        nc.sync.dma_start(xa_sb[0][:], xa_rows[:, 0, :])
+        nc.sync.dma_start(hb_sb[:], hb.rearrange("(p i) o -> p (i o)", i=PACK))
+        nc.sync.dma_start(fk_sb[:], fk.rearrange("(p i) o -> p (i o)", i=PACK))
         nc.sync.dma_start(list_a[:], offs)
-        nc.gpsimd.dma_start(hb_sb[:], hb.rearrange("(p i) o -> p (i o)", i=PACK))
-        nc.gpsimd.dma_start(fk_sb[:], fk.rearrange("(p i) o -> p (i o)", i=PACK))
-        for i in range(1, PACK):
+        for i in range(PACK):
             nc.sync.dma_start(xa_sb[i][:], xa_rows[:, i, :])
         nc.sync.dma_start(w_raw[:], w_words[0])
         nc.sync.dma_start(list_z[:], offs3)
-        nc.sync.dma_start(us_sb[:], us.rearrange("o (p t) -> p (o t)", t=PACK))
         nc.sync.dma_start(
             tz_sb[:].rearrange("p (h z) -> p h z", h=2), tz.rearrange("(h p) z -> p h z", h=2)
         )
         nc.sync.dma_start(wb_sb[:], wb_words[0])
-        load_scale_rows(nc.sync, wbs_sb, wb_scales)
+        load_scale_rows(nc, wbs_sb, wb_scales)
         nc.sync.dma_start(rw_sb[:], rw.to_broadcast([P, J]))
 
-        ws_dealt = sb.tile([P, SLOTS * P], U8, name="ws_dealt", align_bytes=64)
+        us_neg = sb.tile([P, PACK], F32, name="us_neg")
+        nc.scalar.activation(us_neg[:], us_sb[:], COPY, scale=-NEIGHBOUR)
+
+        ws_dealt = sb.tile([P, SETS * P], U8, name="ws_dealt", align_bytes=64)
         nc.vector.memset(ws_dealt[:, 0:4].bitcast(I32), 0)
         nc.vector.tensor_copy(ws_dealt[:, 1:P], ws_raw[:, PACK - 1 : R - PACK : PACK])
         nc.vector.tensor_copy(
@@ -111,8 +114,8 @@ def tile_list_rows_boundedgaps_neighbours_floored_kernel(
         pieces = [(i, 0, J) for i in range(PACK - 1)] + [(PACK - 1, 0, HALF), (PACK - 1, HALF, J)]
         for n, (i, j0, j1) in enumerate(pieces):
             ga = sb.tile([P, j1 - j0], F32, name="ga%d" % n, tag="ga%d" % n, align_bytes=64)
-            window = xa_sb[i][:].indirect(list_a[:, j0 // 16 : j1 // 16])
-            if n in (0, 4):
+            window = xa_sb[i][:].indirect(list_a[:, j0 // LIST_ROWS : j1 // LIST_ROWS])
+            if n == len(pieces) - 1:
                 nc.vector.tensor_copy(ga[:], window)
             else:
                 nc.scalar.activation(ga[:], window, COPY)
@@ -120,7 +123,9 @@ def tile_list_rows_boundedgaps_neighbours_floored_kernel(
                 u_planes[:, i, j0:j1], ga[:], fk_sb[:, i : i + 1], low[i][:, j0:j1], op0=ALU.mult, op1=ALU.subtract
             )
 
-        u_bf = [sb.tile([P, PACK * HALF], BF16, name="u_bf%d" % g, align_bytes=64) for g in range(2)]
+        u_bf = [
+            sb.tile([P, PACK * HALF], BF16, name="u_bf%d" % g, tag="u_bf%d" % g, align_bytes=64) for g in range(2)
+        ]
         u_codes = [sb.tile([P, HALF], U32, name="u_codes%d" % g, align_bytes=64) for g in range(2)]
         u_scales = [sb.tile([P, HALF], U8, name="u_scales%d" % g, align_bytes=64) for g in range(2)]
         for g in range(2):
@@ -128,7 +133,7 @@ def tile_list_rows_boundedgaps_neighbours_floored_kernel(
         for g in range(2):
             nc.vector.quantize_mx(out=u_codes[g][:].bitcast(E4M3), scales=u_scales[g][:], in_=u_bf[g][:])
 
-        w_dealt = sb.tile([P, SLOTS * 2 * P], U8, name="w_dealt", tag="ga3", align_bytes=64)
+        w_dealt = sb.tile([P, SETS * 2 * P], U8, name="w_dealt", tag="ga2", align_bytes=64)
         w16 = w_raw[:].bitcast(U16)
         d16 = w_dealt[:].bitcast(U16)
         nc.scalar.copy(
@@ -138,18 +143,14 @@ def tile_list_rows_boundedgaps_neighbours_floored_kernel(
         nc.gpsimd.memset(w_dealt[:, 0:4].bitcast(I32), 0)
         nc.scalar.copy(d16[:, 1:P], w16[:, PACK - 1 : R - PACK : PACK])
 
-        us_neg = sb.tile([P, PACK], F32, name="us_neg")
-        nc.gpsimd.tensor_scalar(us_neg[:], us_sb[:], -NEIGHBOUR, None, op0=ALU.mult)
+        tz_g = sb.tile([P, 2, J], F32, name="tz_g", tag="u_bf1", align_bytes=64)
+        nc.vector.tensor_copy(tz_g[:, 0, :], tz_sb[:, 0:Z].indirect(list_z[:]))
+        nc.scalar.activation(tz_g[:, 1, :], tz_sb[:, Z : 2 * Z].indirect(list_z[:]), COPY)
 
-        tz_g = sb.tile([P, 2, J], F32, name="tz_g", tag="ga4", align_bytes=64)
-        nc.scalar.activation(tz_g[:, 0, :], tz_sb[:, 0:Z].indirect(list_z[:]), COPY)
-
-        out_rows = out.rearrange("(h p) j -> p h j", h=2)
         acc = []
-        second = []
         for g in range(2):
             banks = [ps.tile([P, 2, HALF], F32, name="first%d_%d" % (g, b)) for b in range(3)]
-            acc.append([banks[(s + 1) // 2][:, s % 2, :] for s in range(SLOTS)])
+            acc.append([banks[(s + 1) // 2][:, s % 2, :] for s in range(SETS)])
             for s in (3, 4, 2, 1, 0):
                 nc.tensor.matmul_mx(
                     out=acc[g][s],
@@ -160,17 +161,17 @@ def tile_list_rows_boundedgaps_neighbours_floored_kernel(
                     start=True,
                     stop=True,
                 )
+
         hid_planes = [sb.tile([P, PACK, HALF], BF16, name="hid_planes%d" % g) for g in range(2)]
         for g in range(2):
             for t in reversed(range(PACK)):
-                if (g, t) == (1, PACK - 1):
-                    before = tz_g[:, 1, 0:HALF]
-                else:
-                    before = sb.tile([P, HALF], F32, name="before%d_%d" % (g, t))[:]
-                nc.scalar.activation(before, acc[g][t], COPY, scale=us_neg[:, t : t + 1])
+                before = sb.tile([P, HALF], F32, name="before%d_%d" % (g, t))
+                nc.scalar.activation(before[:], acc[g][t], COPY, scale=us_neg[:, t : t + 1])
                 nc.vector.scalar_tensor_tensor(
-                    hid_planes[g][:, t, :], acc[g][t + 1], us_sb[:, t : t + 1], before, op0=ALU.mult, op1=ALU.add
+                    hid_planes[g][:, t, :], acc[g][t + 1], us_sb[:, t : t + 1], before[:], op0=ALU.mult, op1=ALU.add
                 )
+
+        second = []
         for g, copy in enumerate((nc.scalar.copy, nc.vector.tensor_copy)):
             hid_bf = sb.tile([P, PACK * HALF], BF16, name="hid_bf%d" % g, tag="hid_bf%d" % g, align_bytes=64)
             hid_codes = sb.tile([P, HALF], U32, name="hid_codes%d" % g, align_bytes=64)
@@ -188,7 +189,8 @@ def tile_list_rows_boundedgaps_neighbours_floored_kernel(
                     start=True,
                     stop=True,
                 )
-        nc.scalar.activation(tz_g[:, 1, :], tz_sb[:, Z : 2 * Z].indirect(list_z[:]), COPY)
+
+        out_rows = out.rearrange("(h p) j -> p h j", h=2)
         for g in range(2):
             top = sb.tile([P, 2, HALF], F32, name="top%d" % g, tag="hid_bf%d" % (1 - g), align_bytes=64)
             y = sb.tile([P, 2, HALF], F32, name="y%d" % g)

from contextlib import ExitStack

import concourse.mybir as mybir

K, T, J, S, R, N, Z = 512, 512, 256, 512, 512, 256, 512
FLOPS = 2 * K * J * R + 2 * R * N * J

F32 = mybir.dt.float32
BF16 = mybir.dt.bfloat16
I32 = mybir.dt.int32
U32 = mybir.dt.uint32
U16 = mybir.dt.uint16
U8 = mybir.dt.uint8
E4M3 = mybir.dt.float8_e4m3fn_x4
E5M2 = mybir.dt.float8_e5m2_x4
E2M1 = mybir.dt.float4_e2m1fn_x4
ALU = mybir.AluOpType
COPY = mybir.ActivationFunctionType.Copy

P = 128
PACK = 4
HALF = J // 2
LIST_ROWS = 16
SETS = PACK + 1
NEIGHBOUR = 0.7


def load_scale_rows(nc, plane, scales):
    rows = scales[0].bitcast(I32)
    for q in range(4):
        four = rows[4 * q : 4 * q + 4, :].unsqueeze(0).to_broadcast([8, 4, rows.shape[1]])
        nc.sync.dma_start(plane[32 * q : 32 * q + 32, :].bitcast(I32), four)


def interleave(copy, packed, planes):
    copy(
        packed.rearrange("p (c e t) -> p c t e", e=4, t=PACK),
        planes.rearrange("p t (c e) -> p c t e", e=4),
    )


def tile_list_rows_boundedgaps_neighbours_floored_kernel(
    tc, xa, xb, hb, fk, w_words, w_scales, us, wb_words, wb_scales, tz, rw, offs, offs2, offs3, out
):
    nc = tc.nc
    with ExitStack() as ctx:
        lists = ctx.enter_context(tc.tile_pool(name="lists", bufs=1))
        sb = ctx.enter_context(tc.tile_pool(name="sb", bufs=1))
        ps = ctx.enter_context(tc.psum_pool(name="ps", bufs=1))
        halves = [slice(g * HALF, (g + 1) * HALF) for g in range(2)]

        list_a = lists.tile([P, J // LIST_ROWS], U16, name="list_a")
        list_b = lists.tile([P, J // LIST_ROWS], U16, name="list_b")
        list_z = lists.tile([P, J // LIST_ROWS], U16, name="list_z")

        xa_rows = xa.rearrange("(p i) t -> p i t", i=PACK)
        xb_rows = xb.rearrange("(p i) s -> p (i s)", i=PACK)
        xa_sb = [sb.tile([P, T], F32, name="xa%d" % i) for i in range(PACK)]
        xb_sb = [sb.tile([P, 2 * S], F32, name="xb%d" % g) for g in range(2)]
        tz_sb = sb.tile([P, 2 * Z], F32, name="tz_sb")
        hb_sb = sb.tile([P, PACK], F32, name="hb_sb")
        fk_sb = sb.tile([P, PACK], F32, name="fk_sb")
        us_sb = sb.tile([P, PACK], F32, name="us_sb")
        rw_sb = sb.tile([P, J], F32, name="rw_sb")
        w_raw = sb.tile([P, 2 * R], U8, name="w_raw", align_bytes=64)
        ws_raw = sb.tile([P, R], U8, name="ws_raw", align_bytes=64)
        wb_sb = sb.tile([P, 2 * N], U8, name="wb_sb", align_bytes=64)
        wbs_sb = sb.tile([P, N], U8, name="wbs_sb", align_bytes=64)

        nc.sync.dma_start(us_sb[:], us.rearrange("o (p t) -> p (o t)", t=PACK))
        nc.sync.dma_start(list_b[:], offs2)
        load_scale_rows(nc, ws_raw, w_scales)
        nc.sync.dma_start(xb_sb[0][:], xb_rows[:, 0 : 2 * S])
        nc.sync.dma_start(xb_sb[1][:], xb_rows[:, 2 * S : 4 * S])
        nc.sync.dma_start(hb_sb[:], hb.rearrange("(p i) o -> p (i o)", i=PACK))
        nc.sync.dma_start(fk_sb[:], fk.rearrange("(p i) o -> p (i o)", i=PACK))
        nc.sync.dma_start(list_a[:], offs)
        for i in range(PACK):
            nc.sync.dma_start(xa_sb[i][:], xa_rows[:, i, :])
        nc.sync.dma_start(w_raw[:], w_words[0])
        nc.sync.dma_start(list_z[:], offs3)
        nc.sync.dma_start(
            tz_sb[:].rearrange("p (h z) -> p h z", h=2), tz.rearrange("(h p) z -> p h z", h=2)
        )
        nc.sync.dma_start(wb_sb[:], wb_words[0])
        load_scale_rows(nc, wbs_sb, wb_scales)
        nc.sync.dma_start(rw_sb[:], rw.to_broadcast([P, J]))

        us_neg = sb.tile([P, PACK], F32, name="us_neg")
        nc.scalar.activation(us_neg[:], us_sb[:], COPY, scale=-NEIGHBOUR)

        ws_dealt = sb.tile([P, SETS * P], U8, name="ws_dealt", align_bytes=64)
        nc.vector.memset(ws_dealt[:, 0:4].bitcast(I32), 0)
        nc.vector.tensor_copy(ws_dealt[:, 1:P], ws_raw[:, PACK - 1 : R - PACK : PACK])
        nc.vector.tensor_copy(
            ws_dealt[:, P:].rearrange("p (t m) -> p t m", t=PACK),
            ws_raw[:].rearrange("p (m t) -> p t m", t=PACK),
        )

        gb = [sb.tile([P, J], F32, name="gb%d" % i) for i in range(PACK)]
        low = [sb.tile([P, J], F32, name="low%d" % i) for i in range(PACK)]
        for i in range(PACK):
            window = xb_sb[i // 2][:, (i % 2) * S : (i % 2 + 1) * S].indirect(list_b[:])
            if i % 2 == 1:
                nc.scalar.activation(gb[i][:], window, COPY)
            else:
                nc.vector.tensor_copy(gb[i][:], window)
        for i in range(PACK):
            nc.vector.tensor_scalar(
                low[i][:], gb[i][:], hb_sb[:, i : i + 1], fk_sb[:, i : i + 1], op0=ALU.min, op1=ALU.mult
            )

        u_planes = sb.tile([P, PACK, J], BF16, name="u_planes")
        pieces = [(i, 0, J) for i in range(PACK - 1)] + [(PACK - 1, 0, HALF), (PACK - 1, HALF, J)]
        for n, (i, j0, j1) in enumerate(pieces):
            ga = sb.tile([P, j1 - j0], F32, name="ga%d" % n, tag="ga%d" % n, align_bytes=64)
            window = xa_sb[i][:].indirect(list_a[:, j0 // LIST_ROWS : j1 // LIST_ROWS])
            if n == len(pieces) - 1:
                nc.vector.tensor_copy(ga[:], window)
            else:
                nc.scalar.activation(ga[:], window, COPY)
            nc.vector.scalar_tensor_tensor(
                u_planes[:, i, j0:j1], ga[:], fk_sb[:, i : i + 1], low[i][:, j0:j1], op0=ALU.mult, op1=ALU.subtract
            )

        u_bf = [
            sb.tile([P, PACK * HALF], BF16, name="u_bf%d" % g, tag="u_bf%d" % g, align_bytes=64) for g in range(2)
        ]
        u_codes = [sb.tile([P, HALF], U32, name="u_codes%d" % g, align_bytes=64) for g in range(2)]
        u_scales = [sb.tile([P, HALF], U8, name="u_scales%d" % g, align_bytes=64) for g in range(2)]
        for g in range(2):
            interleave(nc.vector.tensor_copy, u_bf[g][:], u_planes[:, :, halves[g]])
        for g in range(2):
            nc.vector.quantize_mx(out=u_codes[g][:].bitcast(E4M3), scales=u_scales[g][:], in_=u_bf[g][:])

        w_dealt = sb.tile([P, SETS * 2 * P], U8, name="w_dealt", tag="ga2", align_bytes=64)
        w16 = w_raw[:].bitcast(U16)
        d16 = w_dealt[:].bitcast(U16)
        nc.scalar.copy(
            d16[:, P:].rearrange("p (t m) -> p t m", t=PACK),
            w16.rearrange("p (m t) -> p t m", t=PACK),
        )
        nc.gpsimd.memset(w_dealt[:, 0:4].bitcast(I32), 0)
        nc.scalar.copy(d16[:, 1:P], w16[:, PACK - 1 : R - PACK : PACK])

        tz_g = sb.tile([P, 2, J], F32, name="tz_g", tag="u_bf1", align_bytes=64)
        nc.vector.tensor_copy(tz_g[:, 0, :], tz_sb[:, 0:Z].indirect(list_z[:]))
        nc.scalar.activation(tz_g[:, 1, :], tz_sb[:, Z : 2 * Z].indirect(list_z[:]), COPY)

        acc = []
        for g in range(2):
            banks = [ps.tile([P, 2, HALF], F32, name="first%d_%d" % (g, b)) for b in range(3)]
            acc.append([banks[(s + 1) // 2][:, s % 2, :] for s in range(SETS)])
            for s in (3, 4, 2, 1, 0):
                nc.tensor.matmul_mx(
                    out=acc[g][s],
                    lhsT=w_dealt[:, 2 * P * s : 2 * P * (s + 1)].bitcast(E2M1),
                    lhsT_scale=ws_dealt[:, P * s : P * (s + 1)],
                    rhs=u_codes[g][:].bitcast(E4M3),
                    rhs_scale=u_scales[g][:],
                    start=True,
                    stop=True,
                )

        hid_planes = [sb.tile([P, PACK, HALF], BF16, name="hid_planes%d" % g) for g in range(2)]
        for g in range(2):
            for t in reversed(range(PACK)):
                before = sb.tile([P, HALF], F32, name="before%d_%d" % (g, t))
                nc.scalar.activation(before[:], acc[g][t], COPY, scale=us_neg[:, t : t + 1])
                nc.vector.scalar_tensor_tensor(
                    hid_planes[g][:, t, :], acc[g][t + 1], us_sb[:, t : t + 1], before[:], op0=ALU.mult, op1=ALU.add
                )

        second = []
        for g, copy in enumerate((nc.scalar.copy, nc.vector.tensor_copy)):
            hid_bf = sb.tile([P, PACK * HALF], BF16, name="hid_bf%d" % g, tag="hid_bf%d" % g, align_bytes=64)
            hid_codes = sb.tile([P, HALF], U32, name="hid_codes%d" % g, align_bytes=64)
            hid_scales = sb.tile([P, HALF], U8, name="hid_scales%d" % g, align_bytes=64)
            interleave(copy, hid_bf[:], hid_planes[g][:])
            nc.vector.quantize_mx(out=hid_codes[:].bitcast(E5M2), scales=hid_scales[:], in_=hid_bf[:])
            second.append(ps.tile([P, 2, HALF], F32, name="second%d" % g))
            for h in range(2):
                nc.tensor.matmul_mx(
                    out=second[g][:, h, :],
                    lhsT=wb_sb[:, 2 * P * h : 2 * P * (h + 1)].bitcast(E2M1),
                    lhsT_scale=wbs_sb[:, P * h : P * (h + 1)],
                    rhs=hid_codes[:].bitcast(E5M2),
                    rhs_scale=hid_scales[:],
                    start=True,
                    stop=True,
                )

        out_rows = out.rearrange("(h p) j -> p h j", h=2)
        for g in range(2):
            top = sb.tile([P, 2, HALF], F32, name="top%d" % g, tag="hid_bf%d" % (1 - g), align_bytes=64)
            y = sb.tile([P, 2, HALF], F32, name="y%d" % g)
            nc.vector.tensor_tensor(top[:], second[g][:], tz_g[:, :, halves[g]], ALU.max)
            weight = rw_sb[:, halves[g]].unsqueeze(1).to_broadcast([P, 2, HALF])
            nc.vector.tensor_tensor(y[:], top[:], weight, ALU.mult)
            nc.sync.dma_start(out_rows[:, :, halves[g]], y[:])
